import numpy as np
import ml_dtypes

BF16 = ml_dtypes.bfloat16


def bf(x):
    return np.asarray(x, np.float32).astype(BF16)


def f32(x):
    return np.asarray(x, np.float32)


def f64(x):
    return np.asarray(x).astype(np.float64)


def striped(idx):
    return np.tile(idx.reshape(-1, 16).T, (8, 1))


S, K, M, N, B, Q = 256, 128, 128, 256, 2, 128


def gelu_tanh(v):
    return 0.5 * v * (1.0 + np.tanh(np.sqrt(2.0 / np.pi) * (v + 0.044715 * v**3)))


def setup_inputs():
    return {"base": bf(np.random.standard_normal((B, M, S))), "x": bf(np.random.standard_normal((K, N))), "w": bf(np.random.standard_normal((K, M)) / np.sqrt(K)), "b": f32(0.5 * np.random.standard_normal((M, 1))), "offs": striped(np.random.permutation(S))}


def reference(base, x, w, b, offs):
    idx = offs[:16].T.reshape(-1)
    z = f64(base).copy()
    for i in range(B):
        z[i][:, idx[i * Q : (i + 1) * Q]] = f64(w).T @ f64(x)[:, i * Q : (i + 1) * Q]
    return gelu_tanh(z + f64(b))

@@ -1,0 +1,54 @@
+import concourse.mybir as mybir
+from concourse.masks import make_identity
+
+BF16, F32, U16 = mybir.dt.bfloat16, mybir.dt.float32, mybir.dt.uint16
+GELU = mybir.ActivationFunctionType.Gelu_apprx_tanh
+
+P = 128
+SEQS = 2
+TOKENS = 256
+PIECE = 128
+PIECE_COLS = PIECE // 16
+
+FLOPS = 2 * P * P * SEQS * PIECE
+
+
+def tile_scatter_matmul_kernel(tc, base, x, w, b, offs, out):
+    nc = tc.nc
+    with (
+        tc.tile_pool(name="held", bufs=1) as held,
+        tc.psum_pool(name="banks", bufs=1) as banks,
+    ):
+        offsets = held.tile([P, SEQS * PIECE_COLS], U16, name="offsets")
+        nc.sync.dma_start(offsets[:], offs)
+
+        base_tiles = [held.tile([P, TOKENS], BF16, name="base%d" % i) for i in range(SEQS)]
+        for i in range(SEQS):
+            nc.scalar.dma_start(base_tiles[i][:], base[i])
+        weights = held.tile([P, P], BF16, name="weights")
+        nc.sync.dma_start(weights[:], w)
+        moving = held.tile([P, SEQS * PIECE], BF16, name="moving")
+        nc.sync.dma_start(moving[:], x)
+        bias = held.tile([P, 1], F32, name="bias")
+        nc.scalar.dma_start(bias[:], b)
+
+        identity = held.tile([P, P], BF16, name="identity")
+        make_identity(nc, identity[:])
+
+        windows = [banks.tile([P, TOKENS], F32, name="window%d" % i) for i in range(SEQS)]
+        for i in range(SEQS):
+            nc.tensor.matmul(windows[i][:], identity[:], base_tiles[i][:], start=True, stop=True)
+
+        for i in range(SEQS):
+            nc.tensor.matmul(
+                windows[i][:].indirect(offsets[:, i * PIECE_COLS : (i + 1) * PIECE_COLS]),
+                weights[:],
+                moving[:, i * PIECE : (i + 1) * PIECE],
+                start=True,
+                stop=True,
+            )
+
+        for i in range(SEQS):
+            result = held.tile([P, TOKENS], F32, name="result%d" % i)
+            nc.scalar.activation(result[:], windows[i][:], GELU, bias=bias[:, 0:1])
+            nc.sync.dma_start(out[i], result[:])

@@ -32,6 +32,10 @@ def tile_scatter_matmul_kernel(tc, base, x, w, b, offs, out):
         bias = held.tile([P, 1], F32, name="bias")
         nc.scalar.dma_start(bias[:], b)
 
+        warm = held.tile([P, 1], F32, name="warm")
+        nc.vector.memset(warm[:], 0.0)
+        nc.scalar.activation(warm[:], warm[:], GELU)
+
         identity = held.tile([P, P], BF16, name="identity")
         make_identity(nc, identity[:])
 

@@ -55,4 +55,5 @@ def tile_scatter_matmul_kernel(tc, base, x, w, b, offs, out):
         for i in range(SEQS):
             result = held.tile([P, TOKENS], F32, name="result%d" % i)
             nc.scalar.activation(result[:], windows[i][:], GELU, bias=bias[:, 0:1])
-            nc.sync.dma_start(out[i], result[:])
+            store_queue = nc.scalar if i == SEQS - 1 else nc.sync
+            store_queue.dma_start(out[i], result[:])

import concourse.mybir as mybir
from concourse.masks import make_identity

BF16, F32, U16 = mybir.dt.bfloat16, mybir.dt.float32, mybir.dt.uint16
GELU = mybir.ActivationFunctionType.Gelu_apprx_tanh

P = 128
SEQS = 2
TOKENS = 256
PIECE = 128
PIECE_COLS = PIECE // 16

FLOPS = 2 * P * P * SEQS * PIECE


def tile_scatter_matmul_kernel(tc, base, x, w, b, offs, out):
    nc = tc.nc
    with (
        tc.tile_pool(name="held", bufs=1) as held,
        tc.psum_pool(name="banks", bufs=1) as banks,
    ):
        offsets = held.tile([P, SEQS * PIECE_COLS], U16, name="offsets")
        nc.sync.dma_start(offsets[:], offs)

        base_tiles = [held.tile([P, TOKENS], BF16, name="base%d" % i) for i in range(SEQS)]
        for i in range(SEQS):
            nc.scalar.dma_start(base_tiles[i][:], base[i])
        weights = held.tile([P, P], BF16, name="weights")
        nc.sync.dma_start(weights[:], w)
        moving = held.tile([P, SEQS * PIECE], BF16, name="moving")
        nc.sync.dma_start(moving[:], x)
        bias = held.tile([P, 1], F32, name="bias")
        nc.scalar.dma_start(bias[:], b)

        warm = held.tile([P, 1], F32, name="warm")
        nc.vector.memset(warm[:], 0.0)
        nc.scalar.activation(warm[:], warm[:], GELU)

        identity = held.tile([P, P], BF16, name="identity")
        make_identity(nc, identity[:])

        windows = [banks.tile([P, TOKENS], F32, name="window%d" % i) for i in range(SEQS)]
        for i in range(SEQS):
            nc.tensor.matmul(windows[i][:], identity[:], base_tiles[i][:], start=True, stop=True)

        for i in range(SEQS):
            nc.tensor.matmul(
                windows[i][:].indirect(offsets[:, i * PIECE_COLS : (i + 1) * PIECE_COLS]),
                weights[:],
                moving[:, i * PIECE : (i + 1) * PIECE],
                start=True,
                stop=True,
            )

        for i in range(SEQS):
            result = held.tile([P, TOKENS], F32, name="result%d" % i)
            nc.scalar.activation(result[:], windows[i][:], GELU, bias=bias[:, 0:1])
            store_queue = nc.scalar if i == SEQS - 1 else nc.sync
            store_queue.dma_start(out[i], result[:])
